import numpy as np
import ml_dtypes


def mxq(x, axis, fmt="e4m3"):
    dtype, down = {"e4m3": (ml_dtypes.float8_e4m3fn, 7), "e5m2": (ml_dtypes.float8_e5m2, 14)}[fmt]
    v = np.moveaxis(np.asarray(x, np.float32).astype(ml_dtypes.bfloat16).astype(np.float64), axis, -1)
    blocks = v.reshape(v.shape[:-1] + (-1, 32))
    amax = np.abs(blocks).max(-1, keepdims=True)
    byte = np.maximum(np.where(amax > 0, np.frexp(amax)[1] - 1 + 127, 0) - down, 1)
    scale = np.exp2(byte - 127.0)
    codes = (blocks / scale).astype(np.float32).astype(dtype).astype(np.float64)
    return np.moveaxis((codes * scale).reshape(v.shape), -1, axis)


WIDE = False


def mx_kscale(k):
    if not WIDE:
        return np.ones(k)
    levels = np.array([10, -10, 5, -5, 0])
    if k % 512:
        return np.exp2(np.random.permutation(np.resize(levels, k // 32))).repeat(32)
    a = np.empty((k // 512, 16))
    for p in range(k // 512):
        a[p, :8] = np.random.permutation(np.resize(levels, 8))
        for g in range(8):
            far = levels[np.abs(levels - a[p, g]) >= 10]
            a[p, g + 8] = far[np.random.randint(len(far))]
    return np.exp2(a.ravel()).repeat(32)


def f64(x):
    return np.asarray(x).astype(np.float64)


def striped(idx):
    return np.tile(idx.reshape(-1, 16).T, (8, 1)).astype(np.uint16)


def unstriped(offs):
    return offs[:16].T.reshape(-1).astype(np.int64)


K, T, E, C, N = 512, 1024, 4, 256, 128


def by_expert(wq, xq):
    return np.concatenate([wq[e].T @ xq[:, e * C:(e + 1) * C] for e in range(E)], axis=1)


def setup_inputs():
    n = np.random.standard_normal
    s = mx_kscale(K)[:, None]
    return {
        "xT": (n((K, T)) * s).astype(np.float32),
        "w": (n((E, K, N)) / np.sqrt(K) / s[None]).astype(np.float32),
        "gate": np.tile(np.random.uniform(0.2, 1.0, E * C), (N, 1)).astype(np.float32),
        "offs": striped(np.random.permutation(T)[:E * C]),
    }


def reference(xT, w, gate, offs):
    idx = unstriped(offs)
    xq = mxq(f64(xT)[:, idx], 0, "e4m3")
    y = by_expert(mxq(f64(w), 1, "e4m3"), xq)
    out = np.zeros((N, T))
    out[:, idx] = f64(gate) * y
    return out

@@ -1,0 +1,130 @@
+from contextlib import ExitStack
+
+import concourse.mybir as mybir
+
+K, T, E, C, N = 512, 1024, 4, 256, 128
+FLOPS = 2 * K * N * E * C
+
+F32 = mybir.dt.float32
+BF16 = mybir.dt.bfloat16
+U32 = mybir.dt.uint32
+U16 = mybir.dt.uint16
+U8 = mybir.dt.uint8
+FP8X4 = mybir.dt.float8_e4m3fn_x4
+MULT = mybir.AluOpType.mult
+
+P = 128
+PACK = 4
+HALF = 512
+
+
+def tile_routed_moe_kernel(tc, xT, w, gate, offs, out):
+    nc = tc.nc
+    with ExitStack() as ctx:
+        keep = ctx.enter_context(tc.tile_pool(name="keep", bufs=1))
+        psum = ctx.enter_context(tc.psum_pool(name="psum", bufs=1))
+
+        warm_in = keep.tile([P, 1], F32, name="warm_in")
+        warm_out = keep.tile([P, 1], F32, name="warm_out")
+        nc.gpsimd.memset(warm_in[:], 0.0)
+        nc.scalar.copy(warm_out[:], warm_in[:])
+
+        offsets = keep.tile([P, E * C // 16], U16, name="offsets")
+        nc.sync.dma_start(offsets[:], offs)
+
+        x_view = xT.rearrange("(p t) n -> p t n", t=PACK)
+        w_view = w.rearrange("e (p j) n -> p e j n", j=PACK)
+        planes = [keep.tile([P, T], F32, name="plane%d" % t) for t in range(PACK)]
+        w_raws = [keep.tile([P, 2, PACK, N], F32, name="w_raw%d" % i) for i in range(2)]
+        gate_sb = keep.tile([P, E * C], F32, name="gate_sb")
+        nc.sync.dma_start(planes[0][:], x_view[:, 0, :])
+        nc.sync.dma_start(planes[1][:], x_view[:, 1, :])
+        nc.sync.dma_start(w_raws[0][:], w_view[:, 0:2, :, :])
+        nc.scalar.dma_start(planes[2][:], x_view[:, 2, :])
+        nc.scalar.dma_start(planes[3][:], x_view[:, 3, :])
+        nc.scalar.dma_start(w_raws[1][:], w_view[:, 2:4, :, :])
+        nc.scalar.dma_start(gate_sb[:], gate)
+
+        window = keep.tile([P, T], F32, name="window")
+        w_grouped = keep.tile([P, E, N, PACK], BF16, name="w_grouped", align_bytes=64)
+        w_codes = keep.tile([P, E * N], U32, name="w_codes", align_bytes=64)
+        w_scales = keep.tile([P, E * N], U8, name="w_scales", align_bytes=64)
+
+        def offs_of(first, n):
+            return offsets[:, first // 16 : (first + n) // 16]
+
+        g4 = keep.tile([P, PACK, E * C], F32, name="g4")
+        grouped = [keep.tile([P, C * PACK], BF16, name="grouped%d" % e, align_bytes=64) for e in range(E)]
+        codes = [keep.tile([P, C], U32, name="codes%d" % e, align_bytes=64) for e in range(E)]
+        scales = [keep.tile([P, C], U8, name="scales%d" % e, align_bytes=64) for e in range(E)]
+        accs = [psum.tile([P, C], F32, name="acc%d" % e) for e in range(E)]
+        sums = [keep.tile([P, C], F32, name="sums%d" % e) for e in range(E)]
+
+        def gather(t, first, n):
+            nc.vector.tensor_copy(g4[:, t, first : first + n], planes[t][:].indirect(offs_of(first, n)))
+
+        def interleave(e):
+            nc.scalar.copy(
+                grouped[e][:].rearrange("p (n t) -> p n t", t=PACK),
+                g4[:, :, e * C : (e + 1) * C].rearrange("p t n -> p n t"),
+            )
+
+        def quantize(e):
+            nc.vector.quantize_mx(out=codes[e][:].bitcast(FP8X4), scales=scales[e][:], in_=grouped[e][:])
+
+        def weights(e):
+            nc.scalar.copy(w_grouped[:, e, :, :], w_raws[e // 2][:, e % 2, :, :].rearrange("p j n -> p n j"))
+
+        def quantize_weights():
+            nc.vector.quantize_mx(
+                out=w_codes[:].bitcast(FP8X4),
+                scales=w_scales[:],
+                in_=w_grouped[:].rearrange("p e n j -> p (e n j)"),
+            )
+
+        def multiply(e):
+            nc.tensor.matmul_mx(
+                out=accs[e][:],
+                lhsT=w_codes[:, e * N : (e + 1) * N].bitcast(FP8X4),
+                lhsT_scale=w_scales[:, e * N : (e + 1) * N],
+                rhs=codes[e][:].bitcast(FP8X4),
+                rhs_scale=scales[e][:],
+                start=True,
+                stop=True,
+            )
+            nc.scalar.copy(sums[e][:], accs[e][:])
+
+        def put_back(e):
+            nc.vector.tensor_tensor(
+                window[:].indirect(offs_of(e * C, C)), sums[e][:], gate_sb[:, e * C : (e + 1) * C], MULT
+            )
+
+        gather(0, 0, HALF)
+        gather(0, HALF, HALF)
+        gather(1, 0, HALF)
+        gather(2, 0, HALF)
+        gather(3, 0, HALF)
+        for e in range(E):
+            weights(e)
+        interleave(0)
+        interleave(1)
+        gather(1, HALF, HALF)
+        gather(2, HALF, HALF)
+        quantize_weights()
+        quantize(0)
+        multiply(0)
+        gather(3, HALF, HALF)
+        quantize(1)
+        multiply(1)
+        interleave(2)
+        interleave(3)
+        put_back(0)
+        quantize(2)
+        multiply(2)
+        put_back(1)
+        quantize(3)
+        multiply(3)
+        put_back(2)
+        put_back(3)
+
+        nc.sync.dma_start(out, window[:])

@@ -24,107 +24,105 @@ def tile_routed_moe_kernel(tc, xT, w, gate, offs, out):
         keep = ctx.enter_context(tc.tile_pool(name="keep", bufs=1))
         psum = ctx.enter_context(tc.psum_pool(name="psum", bufs=1))
 
-        warm_in = keep.tile([P, 1], F32, name="warm_in")
-        warm_out = keep.tile([P, 1], F32, name="warm_out")
-        nc.gpsimd.memset(warm_in[:], 0.0)
-        nc.scalar.copy(warm_out[:], warm_in[:])
-
         offsets = keep.tile([P, E * C // 16], U16, name="offsets")
         nc.sync.dma_start(offsets[:], offs)
 
         x_view = xT.rearrange("(p t) n -> p t n", t=PACK)
         w_view = w.rearrange("e (p j) n -> p e j n", j=PACK)
-        planes = [keep.tile([P, T], F32, name="plane%d" % t) for t in range(PACK)]
+        raw = keep.tile([P, PACK, T], F32, name="raw")
         w_raws = [keep.tile([P, 2, PACK, N], F32, name="w_raw%d" % i) for i in range(2)]
         gate_sb = keep.tile([P, E * C], F32, name="gate_sb")
-        nc.sync.dma_start(planes[0][:], x_view[:, 0, :])
-        nc.sync.dma_start(planes[1][:], x_view[:, 1, :])
+        nc.sync.dma_start(raw[:, 0, :], x_view[:, 0, :])
         nc.sync.dma_start(w_raws[0][:], w_view[:, 0:2, :, :])
-        nc.scalar.dma_start(planes[2][:], x_view[:, 2, :])
-        nc.scalar.dma_start(planes[3][:], x_view[:, 3, :])
-        nc.scalar.dma_start(w_raws[1][:], w_view[:, 2:4, :, :])
-        nc.scalar.dma_start(gate_sb[:], gate)
+        nc.sync.dma_start(raw[:, 1, :], x_view[:, 1, :])
+        nc.sync.dma_start(w_raws[1][:], w_view[:, 2:4, :, :])
+        nc.sync.dma_start(raw[:, 2, :], x_view[:, 2, :])
+        nc.sync.dma_start(gate_sb[:], gate)
+        nc.sync.dma_start(raw[:, 3, :], x_view[:, 3, :])
+
+        warm_in = keep.tile([P, 1], F32, name="warm_in")
+        warm_out = keep.tile([P, 1], F32, name="warm_out")
+        nc.gpsimd.memset(warm_in[:], 0.0)
+        nc.scalar.copy(warm_out[:], warm_in[:])
 
         window = keep.tile([P, T], F32, name="window")
-        w_grouped = keep.tile([P, E, N, PACK], BF16, name="w_grouped", align_bytes=64)
-        w_codes = keep.tile([P, E * N], U32, name="w_codes", align_bytes=64)
-        w_scales = keep.tile([P, E * N], U8, name="w_scales", align_bytes=64)
+        w_grouped = [keep.tile([P, 2, N, PACK], BF16, name="w_grouped%d" % i, align_bytes=64) for i in range(2)]
+        w_codes = [keep.tile([P, 2 * N], U32, name="w_codes%d" % i, align_bytes=64) for i in range(2)]
+        w_scales = [keep.tile([P, 2 * N], U8, name="w_scales%d" % i, align_bytes=64) for i in range(2)]
 
         def offs_of(first, n):
             return offsets[:, first // 16 : (first + n) // 16]
 
-        g4 = keep.tile([P, PACK, E * C], F32, name="g4")
-        grouped = [keep.tile([P, C * PACK], BF16, name="grouped%d" % e, align_bytes=64) for e in range(E)]
-        codes = [keep.tile([P, C], U32, name="codes%d" % e, align_bytes=64) for e in range(E)]
-        scales = [keep.tile([P, C], U8, name="scales%d" % e, align_bytes=64) for e in range(E)]
-        accs = [psum.tile([P, C], F32, name="acc%d" % e) for e in range(E)]
-        sums = [keep.tile([P, C], F32, name="sums%d" % e) for e in range(E)]
+        grouped = [keep.tile([P, HALF * PACK], BF16, name="grouped%d" % h, align_bytes=64) for h in range(2)]
+        codes = [keep.tile([P, HALF], U32, name="codes%d" % h, align_bytes=64) for h in range(2)]
+        scales = [keep.tile([P, HALF], U8, name="scales%d" % h, align_bytes=64) for h in range(2)]
+        accs = [psum.tile([P, HALF], F32, name="acc%d" % h) for h in range(2)]
+        sums = [keep.tile([P, HALF], F32, name="sums%d" % h) for h in range(2)]
 
         def gather(t, first, n):
-            nc.vector.tensor_copy(g4[:, t, first : first + n], planes[t][:].indirect(offs_of(first, n)))
-
-        def interleave(e):
-            nc.scalar.copy(
-                grouped[e][:].rearrange("p (n t) -> p n t", t=PACK),
-                g4[:, :, e * C : (e + 1) * C].rearrange("p t n -> p n t"),
+            h, c0 = divmod(first, HALF)
+            nc.vector.tensor_copy(
+                grouped[h][:, c0 * PACK : (c0 + n) * PACK].rearrange("p (n t) -> p n t", t=PACK)[:, :, t],
+                raw[:, t, :].indirect(offs_of(first, n)),
             )
 
         def quantize(e):
-            nc.vector.quantize_mx(out=codes[e][:].bitcast(FP8X4), scales=scales[e][:], in_=grouped[e][:])
+            h, c0 = divmod(e * C, HALF)
+            nc.vector.quantize_mx(
+                out=codes[h][:, c0 : c0 + C].bitcast(FP8X4),
+                scales=scales[h][:, c0 : c0 + C],
+                in_=grouped[h][:, c0 * PACK : (c0 + C) * PACK],
+            )
 
         def weights(e):
-            nc.scalar.copy(w_grouped[:, e, :, :], w_raws[e // 2][:, e % 2, :, :].rearrange("p j n -> p n j"))
+            nc.scalar.copy(w_grouped[e // 2][:, e % 2, :, :], w_raws[e // 2][:, e % 2, :, :].rearrange("p j n -> p n j"))
 
-        def quantize_weights():
+        def quantize_weights(i):
             nc.vector.quantize_mx(
-                out=w_codes[:].bitcast(FP8X4),
-                scales=w_scales[:],
-                in_=w_grouped[:].rearrange("p e n j -> p (e n j)"),
+                out=w_codes[i][:].bitcast(FP8X4),
+                scales=w_scales[i][:],
+                in_=w_grouped[i][:].rearrange("p e n j -> p (e n j)"),
             )
 
         def multiply(e):
+            h, c0 = divmod(e * C, HALF)
+            m0 = (e % 2) * N
             nc.tensor.matmul_mx(
-                out=accs[e][:],
-                lhsT=w_codes[:, e * N : (e + 1) * N].bitcast(FP8X4),
-                lhsT_scale=w_scales[:, e * N : (e + 1) * N],
-                rhs=codes[e][:].bitcast(FP8X4),
-                rhs_scale=scales[e][:],
+                out=accs[h][:, c0 : c0 + C],
+                lhsT=w_codes[e // 2][:, m0 : m0 + N].bitcast(FP8X4),
+                lhsT_scale=w_scales[e // 2][:, m0 : m0 + N],
+                rhs=codes[h][:, c0 : c0 + C].bitcast(FP8X4),
+                rhs_scale=scales[h][:, c0 : c0 + C],
                 start=True,
                 stop=True,
             )
-            nc.scalar.copy(sums[e][:], accs[e][:])
 
-        def put_back(e):
+        def put_back(h):
+            nc.scalar.copy(sums[h][:], accs[h][:])
             nc.vector.tensor_tensor(
-                window[:].indirect(offs_of(e * C, C)), sums[e][:], gate_sb[:, e * C : (e + 1) * C], MULT
+                window[:].indirect(offs_of(h * HALF, HALF)), sums[h][:], gate_sb[:, h * HALF : (h + 1) * HALF], MULT
             )
 
-        gather(0, 0, HALF)
-        gather(0, HALF, HALF)
-        gather(1, 0, HALF)
-        gather(2, 0, HALF)
-        gather(3, 0, HALF)
-        for e in range(E):
-            weights(e)
-        interleave(0)
-        interleave(1)
-        gather(1, HALF, HALF)
-        gather(2, HALF, HALF)
-        quantize_weights()
+        for t in range(3):
+            gather(t, 0, HALF)
+            gather(t, HALF, HALF)
+            if t < 2:
+                weights(2 * t)
+                weights(2 * t + 1)
+                quantize_weights(t)
+        gather(3, 0, C)
+        gather(3, C, C)
         quantize(0)
         multiply(0)
-        gather(3, HALF, HALF)
+        gather(3, 2 * C, C)
         quantize(1)
         multiply(1)
-        interleave(2)
-        interleave(3)
-        put_back(0)
+        gather(3, 3 * C, C)
         quantize(2)
         multiply(2)
-        put_back(1)
         quantize(3)
         multiply(3)
-        put_back(2)
-        put_back(3)
+        put_back(0)
+        put_back(1)
 
         nc.sync.dma_start(out, window[:])

@@ -24,105 +24,109 @@ def tile_routed_moe_kernel(tc, xT, w, gate, offs, out):
         keep = ctx.enter_context(tc.tile_pool(name="keep", bufs=1))
         psum = ctx.enter_context(tc.psum_pool(name="psum", bufs=1))
 
+        held = ("plane2", "plane3", "w_raw1", "gate_sb")
+        warm_out = keep.tile([P, len(held)], F32, name="warm_out")
+        for i, tag in enumerate(held):
+            warm_in = keep.tile([P, 1], F32, name="warm_" + tag, tag=tag)
+            nc.gpsimd.memset(warm_in[:], 0.0)
+            nc.scalar.copy(warm_out[:, i : i + 1], warm_in[:])
+
         offsets = keep.tile([P, E * C // 16], U16, name="offsets")
         nc.sync.dma_start(offsets[:], offs)
 
         x_view = xT.rearrange("(p t) n -> p t n", t=PACK)
         w_view = w.rearrange("e (p j) n -> p e j n", j=PACK)
-        raw = keep.tile([P, PACK, T], F32, name="raw")
-        w_raws = [keep.tile([P, 2, PACK, N], F32, name="w_raw%d" % i) for i in range(2)]
-        gate_sb = keep.tile([P, E * C], F32, name="gate_sb")
-        nc.sync.dma_start(raw[:, 0, :], x_view[:, 0, :])
+        planes = [keep.tile([P, T], F32, name="x_plane%d" % t, tag="plane%d" % t) for t in range(PACK)]
+        w_raws = [keep.tile([P, 2, PACK, N], F32, name="w_rows%d" % i, tag="w_raw%d" % i) for i in range(2)]
+        gate_sb = keep.tile([P, E * C], F32, name="gate_rows", tag="gate_sb")
+        nc.sync.dma_start(planes[0][:], x_view[:, 0, :])
+        nc.sync.dma_start(planes[1][:], x_view[:, 1, :])
         nc.sync.dma_start(w_raws[0][:], w_view[:, 0:2, :, :])
-        nc.sync.dma_start(raw[:, 1, :], x_view[:, 1, :])
-        nc.sync.dma_start(w_raws[1][:], w_view[:, 2:4, :, :])
-        nc.sync.dma_start(raw[:, 2, :], x_view[:, 2, :])
-        nc.sync.dma_start(gate_sb[:], gate)
-        nc.sync.dma_start(raw[:, 3, :], x_view[:, 3, :])
-
-        warm_in = keep.tile([P, 1], F32, name="warm_in")
-        warm_out = keep.tile([P, 1], F32, name="warm_out")
-        nc.gpsimd.memset(warm_in[:], 0.0)
-        nc.scalar.copy(warm_out[:], warm_in[:])
+        nc.scalar.dma_start(planes[2][:], x_view[:, 2, :])
+        nc.scalar.dma_start(planes[3][:], x_view[:, 3, :])
+        nc.scalar.dma_start(w_raws[1][:], w_view[:, 2:4, :, :])
+        nc.scalar.dma_start(gate_sb[:], gate)
 
         window = keep.tile([P, T], F32, name="window")
-        w_grouped = [keep.tile([P, 2, N, PACK], BF16, name="w_grouped%d" % i, align_bytes=64) for i in range(2)]
-        w_codes = [keep.tile([P, 2 * N], U32, name="w_codes%d" % i, align_bytes=64) for i in range(2)]
-        w_scales = [keep.tile([P, 2 * N], U8, name="w_scales%d" % i, align_bytes=64) for i in range(2)]
+        w_grouped = keep.tile([P, E, N, PACK], BF16, name="w_grouped", align_bytes=64)
+        w_codes = keep.tile([P, E * N], U32, name="w_codes", align_bytes=64)
+        w_scales = keep.tile([P, E * N], U8, name="w_scales", align_bytes=64)
 
         def offs_of(first, n):
             return offsets[:, first // 16 : (first + n) // 16]
 
-        grouped = [keep.tile([P, HALF * PACK], BF16, name="grouped%d" % h, align_bytes=64) for h in range(2)]
-        codes = [keep.tile([P, HALF], U32, name="codes%d" % h, align_bytes=64) for h in range(2)]
-        scales = [keep.tile([P, HALF], U8, name="scales%d" % h, align_bytes=64) for h in range(2)]
-        accs = [psum.tile([P, HALF], F32, name="acc%d" % h) for h in range(2)]
-        sums = [keep.tile([P, HALF], F32, name="sums%d" % h) for h in range(2)]
+        g4 = keep.tile([P, PACK, E * C], F32, name="g4")
+        grouped = [keep.tile([P, C * PACK], BF16, name="grouped%d" % e, align_bytes=64) for e in range(E)]
+        codes = [keep.tile([P, C], U32, name="codes%d" % e, align_bytes=64) for e in range(E)]
+        scales = [keep.tile([P, C], U8, name="scales%d" % e, align_bytes=64) for e in range(E)]
+        accs = [psum.tile([P, C], F32, name="acc%d" % e) for e in range(E)]
+        sums = [keep.tile([P, C], F32, name="sums%d" % e) for e in range(E)]
 
         def gather(t, first, n):
-            h, c0 = divmod(first, HALF)
-            nc.vector.tensor_copy(
-                grouped[h][:, c0 * PACK : (c0 + n) * PACK].rearrange("p (n t) -> p n t", t=PACK)[:, :, t],
-                raw[:, t, :].indirect(offs_of(first, n)),
+            nc.vector.tensor_copy(g4[:, t, first : first + n], planes[t][:].indirect(offs_of(first, n)))
+
+        def interleave(e):
+            nc.scalar.copy(
+                grouped[e][:].rearrange("p (n t) -> p n t", t=PACK),
+                g4[:, :, e * C : (e + 1) * C].rearrange("p t n -> p n t"),
             )
 
         def quantize(e):
-            h, c0 = divmod(e * C, HALF)
-            nc.vector.quantize_mx(
-                out=codes[h][:, c0 : c0 + C].bitcast(FP8X4),
-                scales=scales[h][:, c0 : c0 + C],
-                in_=grouped[h][:, c0 * PACK : (c0 + C) * PACK],
-            )
+            nc.vector.quantize_mx(out=codes[e][:].bitcast(FP8X4), scales=scales[e][:], in_=grouped[e][:])
 
         def weights(e):
-            nc.scalar.copy(w_grouped[e // 2][:, e % 2, :, :], w_raws[e // 2][:, e % 2, :, :].rearrange("p j n -> p n j"))
+            nc.scalar.copy(w_grouped[:, e, :, :], w_raws[e // 2][:, e % 2, :, :].rearrange("p j n -> p n j"))
 
-        def quantize_weights(i):
+        def quantize_weights():
             nc.vector.quantize_mx(
-                out=w_codes[i][:].bitcast(FP8X4),
-                scales=w_scales[i][:],
-                in_=w_grouped[i][:].rearrange("p e n j -> p (e n j)"),
+                out=w_codes[:].bitcast(FP8X4),
+                scales=w_scales[:],
+                in_=w_grouped[:].rearrange("p e n j -> p (e n j)"),
             )
 
         def multiply(e):
-            h, c0 = divmod(e * C, HALF)
-            m0 = (e % 2) * N
             nc.tensor.matmul_mx(
-                out=accs[h][:, c0 : c0 + C],
-                lhsT=w_codes[e // 2][:, m0 : m0 + N].bitcast(FP8X4),
-                lhsT_scale=w_scales[e // 2][:, m0 : m0 + N],
-                rhs=codes[h][:, c0 : c0 + C].bitcast(FP8X4),
-                rhs_scale=scales[h][:, c0 : c0 + C],
+                out=accs[e][:],
+                lhsT=w_codes[:, e * N : (e + 1) * N].bitcast(FP8X4),
+                lhsT_scale=w_scales[:, e * N : (e + 1) * N],
+                rhs=codes[e][:].bitcast(FP8X4),
+                rhs_scale=scales[e][:],
                 start=True,
                 stop=True,
             )
+            nc.scalar.copy(sums[e][:], accs[e][:])
 
-        def put_back(h):
-            nc.scalar.copy(sums[h][:], accs[h][:])
+        def put_back(e):
             nc.vector.tensor_tensor(
-                window[:].indirect(offs_of(h * HALF, HALF)), sums[h][:], gate_sb[:, h * HALF : (h + 1) * HALF], MULT
+                window[:].indirect(offs_of(e * C, C)), sums[e][:], gate_sb[:, e * C : (e + 1) * C], MULT
             )
 
-        for t in range(3):
-            gather(t, 0, HALF)
-            gather(t, HALF, HALF)
-            if t < 2:
-                weights(2 * t)
-                weights(2 * t + 1)
-                quantize_weights(t)
-        gather(3, 0, C)
-        gather(3, C, C)
+        gather(0, 0, HALF)
+        gather(0, HALF, HALF)
+        gather(1, 0, HALF)
+        gather(2, 0, HALF)
+        gather(3, 0, HALF)
+        for e in range(E):
+            weights(e)
+        interleave(0)
+        interleave(1)
+        gather(1, HALF, HALF)
+        gather(2, HALF, HALF)
+        quantize_weights()
         quantize(0)
         multiply(0)
-        gather(3, 2 * C, C)
+        gather(3, HALF, HALF)
         quantize(1)
         multiply(1)
-        gather(3, 3 * C, C)
+        interleave(2)
+        interleave(3)
+        put_back(0)
         quantize(2)
         multiply(2)
+        put_back(1)
         quantize(3)
         multiply(3)
-        put_back(0)
-        put_back(1)
+        put_back(2)
+        put_back(3)
 
         nc.sync.dma_start(out, window[:])

@@ -67,15 +67,18 @@ def tile_routed_moe_kernel(tc, xT, w, gate, offs, out):
 
         def interleave(e):
             nc.scalar.copy(
-                grouped[e][:].rearrange("p (n t) -> p n t", t=PACK),
-                g4[:, :, e * C : (e + 1) * C].rearrange("p t n -> p n t"),
+                grouped[e][:].rearrange("p (c i t) -> p c t i", i=4, t=PACK),
+                g4[:, :, e * C : (e + 1) * C].rearrange("p t (c i) -> p c t i", i=4),
             )
 
         def quantize(e):
             nc.vector.quantize_mx(out=codes[e][:].bitcast(FP8X4), scales=scales[e][:], in_=grouped[e][:])
 
         def weights(e):
-            nc.scalar.copy(w_grouped[:, e, :, :], w_raws[e // 2][:, e % 2, :, :].rearrange("p j n -> p n j"))
+            nc.scalar.copy(
+                w_grouped[:, e, :, :].rearrange("p (c i) j -> p c j i", i=4),
+                w_raws[e // 2][:, e % 2, :, :].rearrange("p j (c i) -> p c j i", i=4),
+            )
 
         def quantize_weights():
             nc.vector.quantize_mx(

@@ -12,10 +12,10 @@ U16 = mybir.dt.uint16
 U8 = mybir.dt.uint8
 FP8X4 = mybir.dt.float8_e4m3fn_x4
 MULT = mybir.AluOpType.mult
+COPY = mybir.ActivationFunctionType.Copy
 
 P = 128
 PACK = 4
-HALF = 512
 
 
 def tile_routed_moe_kernel(tc, xT, w, gate, offs, out):
@@ -24,112 +24,135 @@ def tile_routed_moe_kernel(tc, xT, w, gate, offs, out):
         keep = ctx.enter_context(tc.tile_pool(name="keep", bufs=1))
         psum = ctx.enter_context(tc.psum_pool(name="psum", bufs=1))
 
-        held = ("plane2", "plane3", "w_raw1", "gate_sb")
-        warm_out = keep.tile([P, len(held)], F32, name="warm_out")
-        for i, tag in enumerate(held):
-            warm_in = keep.tile([P, 1], F32, name="warm_" + tag, tag=tag)
-            nc.gpsimd.memset(warm_in[:], 0.0)
-            nc.scalar.copy(warm_out[:, i : i + 1], warm_in[:])
+        warm_in = keep.tile([P, 1], F32, name="warm_in")
+        warm_out = keep.tile([P, 1], F32, name="warm_out")
+        nc.gpsimd.memset(warm_in[:], 0.0)
+        nc.scalar.activation(warm_out[:], warm_in[:], COPY)
 
         offsets = keep.tile([P, E * C // 16], U16, name="offsets")
         nc.sync.dma_start(offsets[:], offs)
 
-        x_view = xT.rearrange("(p t) n -> p t n", t=PACK)
-        w_view = w.rearrange("e (p j) n -> p e j n", j=PACK)
-        planes = [keep.tile([P, T], F32, name="x_plane%d" % t, tag="plane%d" % t) for t in range(PACK)]
-        w_raws = [keep.tile([P, 2, PACK, N], F32, name="w_rows%d" % i, tag="w_raw%d" % i) for i in range(2)]
-        gate_sb = keep.tile([P, E * C], F32, name="gate_rows", tag="gate_sb")
-        nc.sync.dma_start(planes[0][:], x_view[:, 0, :])
-        nc.sync.dma_start(planes[1][:], x_view[:, 1, :])
-        nc.sync.dma_start(w_raws[0][:], w_view[:, 0:2, :, :])
-        nc.scalar.dma_start(planes[2][:], x_view[:, 2, :])
-        nc.scalar.dma_start(planes[3][:], x_view[:, 3, :])
-        nc.scalar.dma_start(w_raws[1][:], w_view[:, 2:4, :, :])
-        nc.scalar.dma_start(gate_sb[:], gate)
-
-        window = keep.tile([P, T], F32, name="window")
-        w_grouped = keep.tile([P, E, N, PACK], BF16, name="w_grouped", align_bytes=64)
-        w_codes = keep.tile([P, E * N], U32, name="w_codes", align_bytes=64)
-        w_scales = keep.tile([P, E * N], U8, name="w_scales", align_bytes=64)
-
         def offs_of(first, n):
             return offsets[:, first // 16 : (first + n) // 16]
 
-        g4 = keep.tile([P, PACK, E * C], F32, name="g4")
-        grouped = [keep.tile([P, C * PACK], BF16, name="grouped%d" % e, align_bytes=64) for e in range(E)]
-        codes = [keep.tile([P, C], U32, name="codes%d" % e, align_bytes=64) for e in range(E)]
-        scales = [keep.tile([P, C], U8, name="scales%d" % e, align_bytes=64) for e in range(E)]
-        accs = [psum.tile([P, C], F32, name="acc%d" % e) for e in range(E)]
-        sums = [keep.tile([P, C], F32, name="sums%d" % e) for e in range(E)]
+        x_view = xT.rearrange("(p t) n -> p t n", t=PACK)
+        w_view = w.rearrange("e (p j) n -> p e j n", j=PACK)
+        planes = [
+            keep.tile([P, T], F32, name="x_plane%d" % t, tag=("chain_a" if t == 3 else "x_plane%d" % t), align_bytes=64)
+            for t in range(PACK)
+        ]
+        planes_bf = [keep.tile([P, T], BF16, name="x_bf%d" % t) for t in range(PACK)]
+        w_raw01 = keep.tile([P, 2, PACK, N], F32, name="w_raw01")
+        w_raw23 = keep.tile([P, 2, PACK, N], F32, name="w_raw23", tag="chain_b", align_bytes=64)
+        w_raws = [w_raw01, w_raw23]
+        gate_sb = keep.tile([P, E * C], F32, name="gate_rows")
+        for t in range(PACK):
+            nc.sync.dma_start(planes[t][:], x_view[:, t, :])
+        nc.sync.dma_start(w_raw01[:], w_view[:, 0:2, :, :])
+        nc.sync.dma_start(w_raw23[:], w_view[:, 2:4, :, :])
+        nc.sync.dma_start(gate_sb[:], gate)
 
-        def gather(t, first, n):
-            nc.vector.tensor_copy(g4[:, t, first : first + n], planes[t][:].indirect(offs_of(first, n)))
+        window = keep.tile([P, T], F32, name="window")
+        accs = [psum.tile([P, n], F32, name="acc%d" % c) for c, n in enumerate((C, C, C, C // 2, C // 2))]
 
-        def interleave(e):
-            nc.scalar.copy(
-                grouped[e][:].rearrange("p (c i t) -> p c t i", i=4, t=PACK),
-                g4[:, :, e * C : (e + 1) * C].rearrange("p t (c i) -> p c t i", i=4),
-            )
+        def interleave_weights(engine_copy, i, w_grouped):
+            for h in range(2):
+                engine_copy(
+                    w_grouped[:, h, :, :].rearrange("p (c i) j -> p c j i", i=4),
+                    w_raws[i][:, h, :, :].rearrange("p j (c i) -> p c j i", i=4),
+                )
 
-        def quantize(e):
-            nc.vector.quantize_mx(out=codes[e][:].bitcast(FP8X4), scales=scales[e][:], in_=grouped[e][:])
+        def quantize(codes, scales, grouped):
+            nc.vector.quantize_mx(out=codes.bitcast(FP8X4), scales=scales, in_=grouped)
 
-        def weights(e):
-            nc.scalar.copy(
-                w_grouped[:, e, :, :].rearrange("p (c i) j -> p c j i", i=4),
-                w_raws[e // 2][:, e % 2, :, :].rearrange("p j (c i) -> p c j i", i=4),
-            )
-
-        def quantize_weights():
-            nc.vector.quantize_mx(
-                out=w_codes[:].bitcast(FP8X4),
-                scales=w_scales[:],
-                in_=w_grouped[:].rearrange("p e n j -> p (e n j)"),
-            )
-
-        def multiply(e):
+        def multiply(acc, w_codes, w_scales, h, codes, scales):
             nc.tensor.matmul_mx(
-                out=accs[e][:],
-                lhsT=w_codes[:, e * N : (e + 1) * N].bitcast(FP8X4),
-                lhsT_scale=w_scales[:, e * N : (e + 1) * N],
-                rhs=codes[e][:].bitcast(FP8X4),
-                rhs_scale=scales[e][:],
+                out=acc,
+                lhsT=w_codes[:, h * N : (h + 1) * N].bitcast(FP8X4),
+                lhsT_scale=w_scales[:, h * N : (h + 1) * N],
+                rhs=codes.bitcast(FP8X4),
+                rhs_scale=scales,
                 start=True,
                 stop=True,
             )
-            nc.scalar.copy(sums[e][:], accs[e][:])
 
-        def put_back(e):
-            nc.vector.tensor_tensor(
-                window[:].indirect(offs_of(e * C, C)), sums[e][:], gate_sb[:, e * C : (e + 1) * C], MULT
-            )
+        def scalar_gathers(grouped, first, n):
+            for t in range(PACK):
+                nc.scalar.activation(
+                    grouped.rearrange("p (s t) -> p s t", t=PACK)[:, :, t],
+                    planes_bf[t][:].indirect(offs_of(first, n)),
+                    COPY,
+                )
 
-        gather(0, 0, HALF)
-        gather(0, HALF, HALF)
-        gather(1, 0, HALF)
-        gather(2, 0, HALF)
-        gather(3, 0, HALF)
-        for e in range(E):
-            weights(e)
-        interleave(0)
-        interleave(1)
-        gather(1, HALF, HALF)
-        gather(2, HALF, HALF)
-        quantize_weights()
-        quantize(0)
-        multiply(0)
-        gather(3, HALF, HALF)
-        quantize(1)
-        multiply(1)
-        interleave(2)
-        interleave(3)
-        put_back(0)
-        quantize(2)
-        multiply(2)
-        put_back(1)
-        quantize(3)
-        multiply(3)
-        put_back(2)
-        put_back(3)
+        def put_back(sums, first, n):
+            nc.vector.tensor_tensor(window[:].indirect(offs_of(first, n)), sums, gate_sb[:, first : first + n], MULT)
+
+        g4 = keep.tile([P, PACK, C], F32, name="g4")
+        for t in range(PACK):
+            nc.vector.tensor_copy(planes_bf[t][:], planes[t][:])
+            nc.vector.tensor_copy(g4[:, t, :], planes[t][:].indirect(offs_of(0, C)))
+
+        grouped1 = keep.tile([P, C * PACK], BF16, name="grouped1", align_bytes=64)
+        scalar_gathers(grouped1[:], C, C)
+
+        grouped0 = keep.tile([P, C * PACK], BF16, name="grouped0", align_bytes=64)
+        nc.vector.tensor_copy(
+            grouped0[:].rearrange("p (c i t) -> p c t i", i=4, t=PACK),
+            g4[:].rearrange("p t (c i) -> p c t i", i=4),
+        )
+        w_grouped01 = keep.tile([P, 2, N, PACK], BF16, name="w_grouped01", align_bytes=64)
+        w_codes01 = keep.tile([P, 2 * N], U32, name="w_codes01", align_bytes=64)
+        w_scales01 = keep.tile([P, 2 * N], U8, name="w_scales01", align_bytes=64)
+        interleave_weights(nc.vector.tensor_copy, 0, w_grouped01)
+        quantize(w_codes01[:], w_scales01[:], w_grouped01[:].rearrange("p e n j -> p (e n j)"))
+
+        codes0 = keep.tile([P, C], U32, name="codes0", align_bytes=64)
+        scales0 = keep.tile([P, C], U8, name="scales0", align_bytes=64)
+        quantize(codes0[:], scales0[:], grouped0[:])
+        multiply(accs[0][:], w_codes01, w_scales01, 0, codes0[:], scales0[:])
+        codes1 = keep.tile([P, C], U32, name="codes1", align_bytes=64)
+        scales1 = keep.tile([P, C], U8, name="scales1", align_bytes=64)
+        quantize(codes1[:], scales1[:], grouped1[:])
+        multiply(accs[1][:], w_codes01, w_scales01, 1, codes1[:], scales1[:])
+
+        grouped2 = keep.tile([P, C * PACK], BF16, name="grouped2", tag="chain_a", align_bytes=64)
+        scalar_gathers(grouped2[:], 2 * C, C)
+        w_grouped23 = keep.tile([P, 2, N, PACK], BF16, name="w_grouped23", tag="chain_d", align_bytes=64)
+        interleave_weights(nc.scalar.copy, 1, w_grouped23)
+        grouped3 = keep.tile([P, C * PACK], BF16, name="grouped3", tag="chain_b", align_bytes=64)
+        scalar_gathers(grouped3[:, 0 : C * PACK // 2], 3 * C, C // 2)
+        scalar_gathers(grouped3[:, C * PACK // 2 : C * PACK], 3 * C + C // 2, C // 2)
+
+        sums0 = keep.tile([P, C], F32, name="sums0", tag="chain_c", align_bytes=64)
+        nc.vector.tensor_copy(sums0[:], accs[0][:])
+        put_back(sums0[:], 0, C)
+
+        w_codes23 = keep.tile([P, 2 * N], U32, name="w_codes23", tag="chain_c", align_bytes=64)
+        w_scales23 = keep.tile([P, 2 * N], U8, name="w_scales23", align_bytes=64)
+        quantize(w_codes23[:], w_scales23[:], w_grouped23[:].rearrange("p e n j -> p (e n j)"))
+        codes2 = keep.tile([P, C], U32, name="codes2", tag="chain_d", align_bytes=64)
+        scales2 = keep.tile([P, C], U8, name="scales2", align_bytes=64)
+        quantize(codes2[:], scales2[:], grouped2[:])
+        multiply(accs[2][:], w_codes23, w_scales23, 0, codes2[:], scales2[:])
+
+        sums1 = keep.tile([P, C], F32, name="sums1", tag="chain_a", align_bytes=64)
+        nc.vector.tensor_copy(sums1[:], accs[1][:])
+        put_back(sums1[:], C, C)
+
+        codes3 = keep.tile([P, C], U32, name="codes3", tag="chain_a", align_bytes=64)
+        scales3 = keep.tile([P, C], U8, name="scales3", align_bytes=64)
+        sums2 = keep.tile([P, C], F32, name="sums2")
+        sums3 = keep.tile([P, C], F32, name="sums3")
+        H = C // 2
+        quantize(codes3[:, 0:H], scales3[:, 0:H], grouped3[:, 0 : H * PACK])
+        multiply(accs[3][:], w_codes23, w_scales23, 1, codes3[:, 0:H], scales3[:, 0:H])
+        quantize(codes3[:, H:C], scales3[:, H:C], grouped3[:, H * PACK : C * PACK])
+        multiply(accs[4][:], w_codes23, w_scales23, 1, codes3[:, H:C], scales3[:, H:C])
+        nc.scalar.copy(sums2[:], accs[2][:])
+        put_back(sums2[:], 2 * C, C)
+        nc.scalar.copy(sums3[:, 0:H], accs[3][:])
+        put_back(sums3[:, 0:H], 3 * C, H)
+        nc.scalar.copy(sums3[:, H:C], accs[4][:])
+        put_back(sums3[:, H:C], 3 * C + H, H)
 
         nc.sync.dma_start(out, window[:])

@@ -16,6 +16,7 @@ COPY = mybir.ActivationFunctionType.Copy
 
 P = 128
 PACK = 4
+H = C // 2
 
 
 def tile_routed_moe_kernel(tc, xT, w, gate, offs, out):
@@ -37,13 +38,10 @@ def tile_routed_moe_kernel(tc, xT, w, gate, offs, out):
 
         x_view = xT.rearrange("(p t) n -> p t n", t=PACK)
         w_view = w.rearrange("e (p j) n -> p e j n", j=PACK)
-        planes = [
-            keep.tile([P, T], F32, name="x_plane%d" % t, tag=("chain_a" if t == 3 else "x_plane%d" % t), align_bytes=64)
-            for t in range(PACK)
-        ]
+        planes = [keep.tile([P, T], F32, name="x_plane%d" % t) for t in range(PACK)]
         planes_bf = [keep.tile([P, T], BF16, name="x_bf%d" % t) for t in range(PACK)]
         w_raw01 = keep.tile([P, 2, PACK, N], F32, name="w_raw01")
-        w_raw23 = keep.tile([P, 2, PACK, N], F32, name="w_raw23", tag="chain_b", align_bytes=64)
+        w_raw23 = keep.tile([P, 2, PACK, N], F32, name="w_raw23", tag="after_w23", align_bytes=64)
         w_raws = [w_raw01, w_raw23]
         gate_sb = keep.tile([P, E * C], F32, name="gate_rows")
         for t in range(PACK):
@@ -53,7 +51,6 @@ def tile_routed_moe_kernel(tc, xT, w, gate, offs, out):
         nc.sync.dma_start(gate_sb[:], gate)
 
         window = keep.tile([P, T], F32, name="window")
-        accs = [psum.tile([P, n], F32, name="acc%d" % c) for c, n in enumerate((C, C, C, C // 2, C // 2))]
 
         def interleave_weights(engine_copy, i, w_grouped):
             for h in range(2):
@@ -65,9 +62,10 @@ def tile_routed_moe_kernel(tc, xT, w, gate, offs, out):
         def quantize(codes, scales, grouped):
             nc.vector.quantize_mx(out=codes.bitcast(FP8X4), scales=scales, in_=grouped)
 
-        def multiply(acc, w_codes, w_scales, h, codes, scales):
+        def multiply(name, n, w_codes, w_scales, h, codes, scales):
+            acc = psum.tile([P, n], F32, name=name)
             nc.tensor.matmul_mx(
-                out=acc,
+                out=acc[:],
                 lhsT=w_codes[:, h * N : (h + 1) * N].bitcast(FP8X4),
                 lhsT_scale=w_scales[:, h * N : (h + 1) * N],
                 rhs=codes.bitcast(FP8X4),
@@ -75,32 +73,33 @@ def tile_routed_moe_kernel(tc, xT, w, gate, offs, out):
                 start=True,
                 stop=True,
             )
+            return acc
 
-        def scalar_gathers(grouped, first, n):
-            for t in range(PACK):
-                nc.scalar.activation(
-                    grouped.rearrange("p (s t) -> p s t", t=PACK)[:, :, t],
-                    planes_bf[t][:].indirect(offs_of(first, n)),
-                    COPY,
-                )
+        def scalar_gather(grouped, t, first, n):
+            nc.scalar.activation(
+                grouped.rearrange("p (s t) -> p s t", t=PACK)[:, :, t],
+                planes_bf[t][:].indirect(offs_of(first, n)),
+                COPY,
+            )
 
         def put_back(sums, first, n):
             nc.vector.tensor_tensor(window[:].indirect(offs_of(first, n)), sums, gate_sb[:, first : first + n], MULT)
 
         g4 = keep.tile([P, PACK, C], F32, name="g4")
+        grouped1 = keep.tile([P, C * PACK], BF16, name="grouped1", tag="after_q1", align_bytes=64)
+        grouped3a = keep.tile([P, H * PACK], BF16, name="grouped3a", align_bytes=64)
         for t in range(PACK):
-            nc.vector.tensor_copy(planes_bf[t][:], planes[t][:])
+            (nc.vector).tensor_copy(planes_bf[t][:], planes[t][:])
             nc.vector.tensor_copy(g4[:, t, :], planes[t][:].indirect(offs_of(0, C)))
-
-        grouped1 = keep.tile([P, C * PACK], BF16, name="grouped1", align_bytes=64)
-        scalar_gathers(grouped1[:], C, C)
+            scalar_gather(grouped1[:], t, C, C)
+            scalar_gather(grouped3a[:], t, 3 * C, H)
 
         grouped0 = keep.tile([P, C * PACK], BF16, name="grouped0", align_bytes=64)
         nc.vector.tensor_copy(
             grouped0[:].rearrange("p (c i t) -> p c t i", i=4, t=PACK),
             g4[:].rearrange("p t (c i) -> p c t i", i=4),
         )
-        w_grouped01 = keep.tile([P, 2, N, PACK], BF16, name="w_grouped01", align_bytes=64)
+        w_grouped01 = keep.tile([P, 2, N, PACK], BF16, name="w_grouped01", tag="after_qw01", align_bytes=64)
         w_codes01 = keep.tile([P, 2 * N], U32, name="w_codes01", align_bytes=64)
         w_scales01 = keep.tile([P, 2 * N], U8, name="w_scales01", align_bytes=64)
         interleave_weights(nc.vector.tensor_copy, 0, w_grouped01)
@@ -109,50 +108,52 @@ def tile_routed_moe_kernel(tc, xT, w, gate, offs, out):
         codes0 = keep.tile([P, C], U32, name="codes0", align_bytes=64)
         scales0 = keep.tile([P, C], U8, name="scales0", align_bytes=64)
         quantize(codes0[:], scales0[:], grouped0[:])
-        multiply(accs[0][:], w_codes01, w_scales01, 0, codes0[:], scales0[:])
-        codes1 = keep.tile([P, C], U32, name="codes1", align_bytes=64)
+        acc0 = multiply("acc0", C, w_codes01, w_scales01, 0, codes0[:], scales0[:])
+        codes1 = keep.tile([P, C], U32, name="codes1", tag="after_qw01", align_bytes=64)
         scales1 = keep.tile([P, C], U8, name="scales1", align_bytes=64)
         quantize(codes1[:], scales1[:], grouped1[:])
-        multiply(accs[1][:], w_codes01, w_scales01, 1, codes1[:], scales1[:])
+        acc1 = multiply("acc1", C, w_codes01, w_scales01, 1, codes1[:], scales1[:])
+        codes3a = keep.tile([P, H], U32, name="codes3a", tag="after_q1", align_bytes=64)
+        scales3a = keep.tile([P, H], U8, name="scales3a", align_bytes=64)
+        quantize(codes3a[:], scales3a[:], grouped3a[:])
 
-        grouped2 = keep.tile([P, C * PACK], BF16, name="grouped2", tag="chain_a", align_bytes=64)
-        scalar_gathers(grouped2[:], 2 * C, C)
-        w_grouped23 = keep.tile([P, 2, N, PACK], BF16, name="w_grouped23", tag="chain_d", align_bytes=64)
+        w_grouped23 = keep.tile([P, 2, N, PACK], BF16, name="w_grouped23", align_bytes=64)
         interleave_weights(nc.scalar.copy, 1, w_grouped23)
-        grouped3 = keep.tile([P, C * PACK], BF16, name="grouped3", tag="chain_b", align_bytes=64)
-        scalar_gathers(grouped3[:, 0 : C * PACK // 2], 3 * C, C // 2)
-        scalar_gathers(grouped3[:, C * PACK // 2 : C * PACK], 3 * C + C // 2, C // 2)
+        late = keep.tile([P, (C + H) * PACK], BF16, name="grouped_late", tag="after_w23", align_bytes=64)
+        grouped2 = late[:, 0 : C * PACK]
+        grouped3b = late[:, C * PACK : (C + H) * PACK]
+        for t in range(PACK):
+            scalar_gather(grouped2, t, 2 * C, C)
 
-        sums0 = keep.tile([P, C], F32, name="sums0", tag="chain_c", align_bytes=64)
-        nc.vector.tensor_copy(sums0[:], accs[0][:])
-        put_back(sums0[:], 0, C)
-
-        w_codes23 = keep.tile([P, 2 * N], U32, name="w_codes23", tag="chain_c", align_bytes=64)
+        sums0 = keep.tile([P, C], F32, name="sums0")
+        nc.vector.tensor_copy(sums0[:], acc0[:])
+        w_codes23 = keep.tile([P, 2 * N], U32, name="w_codes23", align_bytes=64)
         w_scales23 = keep.tile([P, 2 * N], U8, name="w_scales23", align_bytes=64)
         quantize(w_codes23[:], w_scales23[:], w_grouped23[:].rearrange("p e n j -> p (e n j)"))
-        codes2 = keep.tile([P, C], U32, name="codes2", tag="chain_d", align_bytes=64)
-        scales2 = keep.tile([P, C], U8, name="scales2", align_bytes=64)
-        quantize(codes2[:], scales2[:], grouped2[:])
-        multiply(accs[2][:], w_codes23, w_scales23, 0, codes2[:], scales2[:])
-
-        sums1 = keep.tile([P, C], F32, name="sums1", tag="chain_a", align_bytes=64)
-        nc.vector.tensor_copy(sums1[:], accs[1][:])
+        acc3a = multiply("acc3a", H, w_codes23, w_scales23, 1, codes3a[:], scales3a[:])
+        put_back(sums0[:], 0, C)
+        sums1 = keep.tile([P, C], F32, name="sums1", tag="after_sc1", align_bytes=64)
+        nc.vector.tensor_copy(sums1[:], acc1[:])
+        sums3a = keep.tile([P, H], F32, name="sums3a", tag="after_sc3a", align_bytes=64)
+        nc.scalar.copy(sums3a[:], acc3a[:])
+        for t in range(PACK):
+            scalar_gather(grouped3b, t, 3 * C + H, H)
         put_back(sums1[:], C, C)
 
-        codes3 = keep.tile([P, C], U32, name="codes3", tag="chain_a", align_bytes=64)
-        scales3 = keep.tile([P, C], U8, name="scales3", align_bytes=64)
+        codes2 = keep.tile([P, C], U32, name="codes2", tag="after_sc1", align_bytes=64)
+        scales2 = keep.tile([P, C], U8, name="scales2", align_bytes=64)
+        quantize(codes2[:], scales2[:], grouped2)
+        acc2 = multiply("acc2", C, w_codes23, w_scales23, 0, codes2[:], scales2[:])
+        put_back(sums3a[:], 3 * C, H)
+        codes3b = keep.tile([P, H], U32, name="codes3b", tag="after_sc3a", align_bytes=64)
+        scales3b = keep.tile([P, H], U8, name="scales3b", align_bytes=64)
+        quantize(codes3b[:], scales3b[:], grouped3b)
+        acc3b = multiply("acc3b", H, w_codes23, w_scales23, 1, codes3b[:], scales3b[:])
         sums2 = keep.tile([P, C], F32, name="sums2")
-        sums3 = keep.tile([P, C], F32, name="sums3")
-        H = C // 2
-        quantize(codes3[:, 0:H], scales3[:, 0:H], grouped3[:, 0 : H * PACK])
-        multiply(accs[3][:], w_codes23, w_scales23, 1, codes3[:, 0:H], scales3[:, 0:H])
-        quantize(codes3[:, H:C], scales3[:, H:C], grouped3[:, H * PACK : C * PACK])
-        multiply(accs[4][:], w_codes23, w_scales23, 1, codes3[:, H:C], scales3[:, H:C])
-        nc.scalar.copy(sums2[:], accs[2][:])
+        nc.scalar.copy(sums2[:], acc2[:])
         put_back(sums2[:], 2 * C, C)
-        nc.scalar.copy(sums3[:, 0:H], accs[3][:])
-        put_back(sums3[:, 0:H], 3 * C, H)
-        nc.scalar.copy(sums3[:, H:C], accs[4][:])
-        put_back(sums3[:, H:C], 3 * C + H, H)
+        sums3b = keep.tile([P, H], F32, name="sums3b")
+        nc.scalar.copy(sums3b[:], acc3b[:])
+        put_back(sums3b[:], 3 * C + H, H)
 
         nc.sync.dma_start(out, window[:])

@@ -52,8 +52,8 @@ def tile_routed_moe_kernel(tc, xT, w, gate, offs, out):
 
         window = keep.tile([P, T], F32, name="window")
 
-        def interleave_weights(engine_copy, i, w_grouped):
-            for h in range(2):
+        def interleave_weights(engine_copies, i, w_grouped):
+            for h, engine_copy in enumerate(engine_copies):
                 engine_copy(
                     w_grouped[:, h, :, :].rearrange("p (c i) j -> p c j i", i=4),
                     w_raws[i][:, h, :, :].rearrange("p j (c i) -> p c j i", i=4),
@@ -102,7 +102,7 @@ def tile_routed_moe_kernel(tc, xT, w, gate, offs, out):
         w_grouped01 = keep.tile([P, 2, N, PACK], BF16, name="w_grouped01", tag="after_qw01", align_bytes=64)
         w_codes01 = keep.tile([P, 2 * N], U32, name="w_codes01", align_bytes=64)
         w_scales01 = keep.tile([P, 2 * N], U8, name="w_scales01", align_bytes=64)
-        interleave_weights(nc.vector.tensor_copy, 0, w_grouped01)
+        interleave_weights((nc.vector.tensor_copy, nc.vector.tensor_copy), 0, w_grouped01)
         quantize(w_codes01[:], w_scales01[:], w_grouped01[:].rearrange("p e n j -> p (e n j)"))
 
         codes0 = keep.tile([P, C], U32, name="codes0", align_bytes=64)
@@ -118,22 +118,23 @@ def tile_routed_moe_kernel(tc, xT, w, gate, offs, out):
         quantize(codes3a[:], scales3a[:], grouped3a[:])
 
         w_grouped23 = keep.tile([P, 2, N, PACK], BF16, name="w_grouped23", align_bytes=64)
-        interleave_weights(nc.scalar.copy, 1, w_grouped23)
+        interleave_weights((nc.vector.tensor_copy, nc.scalar.copy), 1, w_grouped23)
         late = keep.tile([P, (C + H) * PACK], BF16, name="grouped_late", tag="after_w23", align_bytes=64)
         grouped2 = late[:, 0 : C * PACK]
         grouped3b = late[:, C * PACK : (C + H) * PACK]
-        for t in range(PACK):
+        sums0 = keep.tile([P, C], F32, name="sums0")
+        nc.scalar.copy(sums0[:], acc0[:])
+        scalar_gather(grouped2, 0, 2 * C, C)
+        sums1 = keep.tile([P, C], F32, name="sums1", tag="after_sc1", align_bytes=64)
+        nc.scalar.copy(sums1[:], acc1[:])
+        for t in range(1, PACK):
             scalar_gather(grouped2, t, 2 * C, C)
 
-        sums0 = keep.tile([P, C], F32, name="sums0")
-        nc.vector.tensor_copy(sums0[:], acc0[:])
         w_codes23 = keep.tile([P, 2 * N], U32, name="w_codes23", align_bytes=64)
         w_scales23 = keep.tile([P, 2 * N], U8, name="w_scales23", align_bytes=64)
         quantize(w_codes23[:], w_scales23[:], w_grouped23[:].rearrange("p e n j -> p (e n j)"))
         acc3a = multiply("acc3a", H, w_codes23, w_scales23, 1, codes3a[:], scales3a[:])
         put_back(sums0[:], 0, C)
-        sums1 = keep.tile([P, C], F32, name="sums1", tag="after_sc1", align_bytes=64)
-        nc.vector.tensor_copy(sums1[:], acc1[:])
         sums3a = keep.tile([P, H], F32, name="sums3a", tag="after_sc3a", align_bytes=64)
         nc.scalar.copy(sums3a[:], acc3a[:])
         for t in range(PACK):

@@ -52,8 +52,8 @@ def tile_routed_moe_kernel(tc, xT, w, gate, offs, out):
 
         window = keep.tile([P, T], F32, name="window")
 
-        def interleave_weights(engine_copies, i, w_grouped):
-            for h, engine_copy in enumerate(engine_copies):
+        def interleave_weights(engine_copy, i, w_grouped):
+            for h in range(2):
                 engine_copy(
                     w_grouped[:, h, :, :].rearrange("p (c i) j -> p c j i", i=4),
                     w_raws[i][:, h, :, :].rearrange("p j (c i) -> p c j i", i=4),
@@ -102,7 +102,7 @@ def tile_routed_moe_kernel(tc, xT, w, gate, offs, out):
         w_grouped01 = keep.tile([P, 2, N, PACK], BF16, name="w_grouped01", tag="after_qw01", align_bytes=64)
         w_codes01 = keep.tile([P, 2 * N], U32, name="w_codes01", align_bytes=64)
         w_scales01 = keep.tile([P, 2 * N], U8, name="w_scales01", align_bytes=64)
-        interleave_weights((nc.vector.tensor_copy, nc.vector.tensor_copy), 0, w_grouped01)
+        interleave_weights(nc.vector.tensor_copy, 0, w_grouped01)
         quantize(w_codes01[:], w_scales01[:], w_grouped01[:].rearrange("p e n j -> p (e n j)"))
 
         codes0 = keep.tile([P, C], U32, name="codes0", align_bytes=64)
@@ -118,7 +118,7 @@ def tile_routed_moe_kernel(tc, xT, w, gate, offs, out):
         quantize(codes3a[:], scales3a[:], grouped3a[:])
 
         w_grouped23 = keep.tile([P, 2, N, PACK], BF16, name="w_grouped23", align_bytes=64)
-        interleave_weights((nc.vector.tensor_copy, nc.scalar.copy), 1, w_grouped23)
+        interleave_weights(nc.scalar.copy, 1, w_grouped23)
         late = keep.tile([P, (C + H) * PACK], BF16, name="grouped_late", tag="after_w23", align_bytes=64)
         grouped2 = late[:, 0 : C * PACK]
         grouped3b = late[:, C * PACK : (C + H) * PACK]

@@ -41,22 +41,24 @@ def tile_routed_moe_kernel(tc, xT, w, gate, offs, out):
         planes = [keep.tile([P, T], F32, name="x_plane%d" % t) for t in range(PACK)]
         planes_bf = [keep.tile([P, T], BF16, name="x_bf%d" % t) for t in range(PACK)]
         w_raw01 = keep.tile([P, 2, PACK, N], F32, name="w_raw01")
-        w_raw23 = keep.tile([P, 2, PACK, N], F32, name="w_raw23", tag="after_w23", align_bytes=64)
-        w_raws = [w_raw01, w_raw23]
+        w_raw2 = keep.tile([P, PACK, N], F32, name="w_raw2")
+        w_raw3 = keep.tile([P, PACK, N], F32, name="w_raw3", tag="after_w3", align_bytes=64)
+        w_rows = [w_raw01[:, 0, :, :], w_raw01[:, 1, :, :], w_raw2[:], w_raw3[:]]
         gate_sb = keep.tile([P, E * C], F32, name="gate_rows")
         for t in range(PACK):
             nc.sync.dma_start(planes[t][:], x_view[:, t, :])
         nc.sync.dma_start(w_raw01[:], w_view[:, 0:2, :, :])
-        nc.sync.dma_start(w_raw23[:], w_view[:, 2:4, :, :])
+        nc.sync.dma_start(w_raw2[:], w_view[:, 2, :, :])
+        nc.sync.dma_start(w_raw3[:], w_view[:, 3, :, :])
         nc.sync.dma_start(gate_sb[:], gate)
 
         window = keep.tile([P, T], F32, name="window")
 
-        def interleave_weights(engine_copy, i, w_grouped):
-            for h in range(2):
+        def interleave_weights(engine_copies, i, w_grouped):
+            for h, engine_copy in enumerate(engine_copies):
                 engine_copy(
                     w_grouped[:, h, :, :].rearrange("p (c i) j -> p c j i", i=4),
-                    w_raws[i][:, h, :, :].rearrange("p j (c i) -> p c j i", i=4),
+                    w_rows[2 * i + h].rearrange("p j (c i) -> p c j i", i=4),
                 )
 
         def quantize(codes, scales, grouped):
@@ -102,7 +104,7 @@ def tile_routed_moe_kernel(tc, xT, w, gate, offs, out):
         w_grouped01 = keep.tile([P, 2, N, PACK], BF16, name="w_grouped01", tag="after_qw01", align_bytes=64)
         w_codes01 = keep.tile([P, 2 * N], U32, name="w_codes01", align_bytes=64)
         w_scales01 = keep.tile([P, 2 * N], U8, name="w_scales01", align_bytes=64)
-        interleave_weights(nc.vector.tensor_copy, 0, w_grouped01)
+        interleave_weights((nc.vector.tensor_copy, nc.vector.tensor_copy), 0, w_grouped01)
         quantize(w_codes01[:], w_scales01[:], w_grouped01[:].rearrange("p e n j -> p (e n j)"))
 
         codes0 = keep.tile([P, C], U32, name="codes0", align_bytes=64)
@@ -118,12 +120,12 @@ def tile_routed_moe_kernel(tc, xT, w, gate, offs, out):
         quantize(codes3a[:], scales3a[:], grouped3a[:])
 
         w_grouped23 = keep.tile([P, 2, N, PACK], BF16, name="w_grouped23", align_bytes=64)
-        interleave_weights(nc.scalar.copy, 1, w_grouped23)
-        late = keep.tile([P, (C + H) * PACK], BF16, name="grouped_late", tag="after_w23", align_bytes=64)
+        interleave_weights((nc.vector.tensor_copy, nc.scalar.copy), 1, w_grouped23)
+        late = keep.tile([P, (C + H) * PACK], BF16, name="grouped_late", tag="after_w3", align_bytes=64)
         grouped2 = late[:, 0 : C * PACK]
         grouped3b = late[:, C * PACK : (C + H) * PACK]
-        sums0 = keep.tile([P, C], F32, name="sums0")
-        nc.scalar.copy(sums0[:], acc0[:])
+        sums0 = keep.tile([P, C], F32, name="sums0", tag="after_sc0", align_bytes=64)
+        nc.vector.tensor_copy(sums0[:], acc0[:])
         scalar_gather(grouped2, 0, 2 * C, C)
         sums1 = keep.tile([P, C], F32, name="sums1", tag="after_sc1", align_bytes=64)
         nc.scalar.copy(sums1[:], acc1[:])
@@ -135,18 +137,18 @@ def tile_routed_moe_kernel(tc, xT, w, gate, offs, out):
         quantize(w_codes23[:], w_scales23[:], w_grouped23[:].rearrange("p e n j -> p (e n j)"))
         acc3a = multiply("acc3a", H, w_codes23, w_scales23, 1, codes3a[:], scales3a[:])
         put_back(sums0[:], 0, C)
-        sums3a = keep.tile([P, H], F32, name="sums3a", tag="after_sc3a", align_bytes=64)
+        sums3a = keep.tile([P, H], F32, name="sums3a")
         nc.scalar.copy(sums3a[:], acc3a[:])
         for t in range(PACK):
             scalar_gather(grouped3b, t, 3 * C + H, H)
         put_back(sums1[:], C, C)
 
-        codes2 = keep.tile([P, C], U32, name="codes2", tag="after_sc1", align_bytes=64)
+        codes2 = keep.tile([P, C], U32, name="codes2", tag="after_sc0", align_bytes=64)
         scales2 = keep.tile([P, C], U8, name="scales2", align_bytes=64)
         quantize(codes2[:], scales2[:], grouped2)
         acc2 = multiply("acc2", C, w_codes23, w_scales23, 0, codes2[:], scales2[:])
         put_back(sums3a[:], 3 * C, H)
-        codes3b = keep.tile([P, H], U32, name="codes3b", tag="after_sc3a", align_bytes=64)
+        codes3b = keep.tile([P, H], U32, name="codes3b", tag="after_sc1", align_bytes=64)
         scales3b = keep.tile([P, H], U8, name="scales3b", align_bytes=64)
         quantize(codes3b[:], scales3b[:], grouped3b)
         acc3b = multiply("acc3b", H, w_codes23, w_scales23, 1, codes3b[:], scales3b[:])

@@ -101,20 +101,28 @@ def tile_routed_moe_kernel(tc, xT, w, gate, offs, out):
             grouped0[:].rearrange("p (c i t) -> p c t i", i=4, t=PACK),
             g4[:].rearrange("p t (c i) -> p c t i", i=4),
         )
-        w_grouped01 = keep.tile([P, 2, N, PACK], BF16, name="w_grouped01", tag="after_qw01", align_bytes=64)
-        w_codes01 = keep.tile([P, 2 * N], U32, name="w_codes01", align_bytes=64)
-        w_scales01 = keep.tile([P, 2 * N], U8, name="w_scales01", align_bytes=64)
-        interleave_weights((nc.vector.tensor_copy, nc.vector.tensor_copy), 0, w_grouped01)
-        quantize(w_codes01[:], w_scales01[:], w_grouped01[:].rearrange("p e n j -> p (e n j)"))
+        w_grouped0 = keep.tile([P, 1, N, PACK], BF16, name="w_grouped0", align_bytes=64)
+        w_codes0 = keep.tile([P, N], U32, name="w_codes0", align_bytes=64)
+        w_scales0 = keep.tile([P, N], U8, name="w_scales0", align_bytes=64)
+        interleave_weights((nc.vector.tensor_copy,), 0, w_grouped0)
+        quantize(w_codes0[:], w_scales0[:], w_grouped0[:].rearrange("p e n j -> p (e n j)"))
 
         codes0 = keep.tile([P, C], U32, name="codes0", align_bytes=64)
         scales0 = keep.tile([P, C], U8, name="scales0", align_bytes=64)
         quantize(codes0[:], scales0[:], grouped0[:])
-        acc0 = multiply("acc0", C, w_codes01, w_scales01, 0, codes0[:], scales0[:])
+        acc0 = multiply("acc0", C, w_codes0, w_scales0, 0, codes0[:], scales0[:])
+        w_grouped1 = keep.tile([P, 1, N, PACK], BF16, name="w_grouped1", tag="after_qw01", align_bytes=64)
+        w_codes1 = keep.tile([P, N], U32, name="w_codes1", align_bytes=64)
+        w_scales1 = keep.tile([P, N], U8, name="w_scales1", align_bytes=64)
+        nc.vector.tensor_copy(
+            w_grouped1[:, 0, :, :].rearrange("p (c i) j -> p c j i", i=4),
+            w_rows[1].rearrange("p j (c i) -> p c j i", i=4),
+        )
+        quantize(w_codes1[:], w_scales1[:], w_grouped1[:].rearrange("p e n j -> p (e n j)"))
         codes1 = keep.tile([P, C], U32, name="codes1", tag="after_qw01", align_bytes=64)
         scales1 = keep.tile([P, C], U8, name="scales1", align_bytes=64)
         quantize(codes1[:], scales1[:], grouped1[:])
-        acc1 = multiply("acc1", C, w_codes01, w_scales01, 1, codes1[:], scales1[:])
+        acc1 = multiply("acc1", C, w_codes1, w_scales1, 0, codes1[:], scales1[:])
         codes3a = keep.tile([P, H], U32, name="codes3a", tag="after_q1", align_bytes=64)
         scales3a = keep.tile([P, H], U8, name="scales3a", align_bytes=64)
         quantize(codes3a[:], scales3a[:], grouped3a[:])

from contextlib import ExitStack

import concourse.mybir as mybir

K, T, E, C, N = 512, 1024, 4, 256, 128
FLOPS = 2 * K * N * E * C

F32 = mybir.dt.float32
BF16 = mybir.dt.bfloat16
U32 = mybir.dt.uint32
U16 = mybir.dt.uint16
U8 = mybir.dt.uint8
FP8X4 = mybir.dt.float8_e4m3fn_x4
MULT = mybir.AluOpType.mult
COPY = mybir.ActivationFunctionType.Copy

P = 128
PACK = 4
H = C // 2


def tile_routed_moe_kernel(tc, xT, w, gate, offs, out):
    nc = tc.nc
    with ExitStack() as ctx:
        keep = ctx.enter_context(tc.tile_pool(name="keep", bufs=1))
        psum = ctx.enter_context(tc.psum_pool(name="psum", bufs=1))

        warm_in = keep.tile([P, 1], F32, name="warm_in")
        warm_out = keep.tile([P, 1], F32, name="warm_out")
        nc.gpsimd.memset(warm_in[:], 0.0)
        nc.scalar.activation(warm_out[:], warm_in[:], COPY)

        offsets = keep.tile([P, E * C // 16], U16, name="offsets")
        nc.sync.dma_start(offsets[:], offs)

        def offs_of(first, n):
            return offsets[:, first // 16 : (first + n) // 16]

        x_view = xT.rearrange("(p t) n -> p t n", t=PACK)
        w_view = w.rearrange("e (p j) n -> p e j n", j=PACK)
        planes = [keep.tile([P, T], F32, name="x_plane%d" % t) for t in range(PACK)]
        planes_bf = [keep.tile([P, T], BF16, name="x_bf%d" % t) for t in range(PACK)]
        w_raw01 = keep.tile([P, 2, PACK, N], F32, name="w_raw01")
        w_raw2 = keep.tile([P, PACK, N], F32, name="w_raw2")
        w_raw3 = keep.tile([P, PACK, N], F32, name="w_raw3", tag="after_w3", align_bytes=64)
        w_rows = [w_raw01[:, 0, :, :], w_raw01[:, 1, :, :], w_raw2[:], w_raw3[:]]
        gate_sb = keep.tile([P, E * C], F32, name="gate_rows")
        for t in range(PACK):
            nc.sync.dma_start(planes[t][:], x_view[:, t, :])
        nc.sync.dma_start(w_raw01[:], w_view[:, 0:2, :, :])
        nc.sync.dma_start(w_raw2[:], w_view[:, 2, :, :])
        nc.sync.dma_start(w_raw3[:], w_view[:, 3, :, :])
        nc.sync.dma_start(gate_sb[:], gate)

        window = keep.tile([P, T], F32, name="window")

        def interleave_weights(engine_copies, i, w_grouped):
            for h, engine_copy in enumerate(engine_copies):
                engine_copy(
                    w_grouped[:, h, :, :].rearrange("p (c i) j -> p c j i", i=4),
                    w_rows[2 * i + h].rearrange("p j (c i) -> p c j i", i=4),
                )

        def quantize(codes, scales, grouped):
            nc.vector.quantize_mx(out=codes.bitcast(FP8X4), scales=scales, in_=grouped)

        def multiply(name, n, w_codes, w_scales, h, codes, scales):
            acc = psum.tile([P, n], F32, name=name)
            nc.tensor.matmul_mx(
                out=acc[:],
                lhsT=w_codes[:, h * N : (h + 1) * N].bitcast(FP8X4),
                lhsT_scale=w_scales[:, h * N : (h + 1) * N],
                rhs=codes.bitcast(FP8X4),
                rhs_scale=scales,
                start=True,
                stop=True,
            )
            return acc

        def scalar_gather(grouped, t, first, n):
            nc.scalar.activation(
                grouped.rearrange("p (s t) -> p s t", t=PACK)[:, :, t],
                planes_bf[t][:].indirect(offs_of(first, n)),
                COPY,
            )

        def put_back(sums, first, n):
            nc.vector.tensor_tensor(window[:].indirect(offs_of(first, n)), sums, gate_sb[:, first : first + n], MULT)

        g4 = keep.tile([P, PACK, C], F32, name="g4")
        grouped1 = keep.tile([P, C * PACK], BF16, name="grouped1", tag="after_q1", align_bytes=64)
        grouped3a = keep.tile([P, H * PACK], BF16, name="grouped3a", align_bytes=64)
        for t in range(PACK):
            (nc.vector).tensor_copy(planes_bf[t][:], planes[t][:])
            nc.vector.tensor_copy(g4[:, t, :], planes[t][:].indirect(offs_of(0, C)))
            scalar_gather(grouped1[:], t, C, C)
            scalar_gather(grouped3a[:], t, 3 * C, H)

        grouped0 = keep.tile([P, C * PACK], BF16, name="grouped0", align_bytes=64)
        nc.vector.tensor_copy(
            grouped0[:].rearrange("p (c i t) -> p c t i", i=4, t=PACK),
            g4[:].rearrange("p t (c i) -> p c t i", i=4),
        )
        w_grouped0 = keep.tile([P, 1, N, PACK], BF16, name="w_grouped0", align_bytes=64)
        w_codes0 = keep.tile([P, N], U32, name="w_codes0", align_bytes=64)
        w_scales0 = keep.tile([P, N], U8, name="w_scales0", align_bytes=64)
        interleave_weights((nc.vector.tensor_copy,), 0, w_grouped0)
        quantize(w_codes0[:], w_scales0[:], w_grouped0[:].rearrange("p e n j -> p (e n j)"))

        codes0 = keep.tile([P, C], U32, name="codes0", align_bytes=64)
        scales0 = keep.tile([P, C], U8, name="scales0", align_bytes=64)
        quantize(codes0[:], scales0[:], grouped0[:])
        acc0 = multiply("acc0", C, w_codes0, w_scales0, 0, codes0[:], scales0[:])
        w_grouped1 = keep.tile([P, 1, N, PACK], BF16, name="w_grouped1", tag="after_qw01", align_bytes=64)
        w_codes1 = keep.tile([P, N], U32, name="w_codes1", align_bytes=64)
        w_scales1 = keep.tile([P, N], U8, name="w_scales1", align_bytes=64)
        nc.vector.tensor_copy(
            w_grouped1[:, 0, :, :].rearrange("p (c i) j -> p c j i", i=4),
            w_rows[1].rearrange("p j (c i) -> p c j i", i=4),
        )
        quantize(w_codes1[:], w_scales1[:], w_grouped1[:].rearrange("p e n j -> p (e n j)"))
        codes1 = keep.tile([P, C], U32, name="codes1", tag="after_qw01", align_bytes=64)
        scales1 = keep.tile([P, C], U8, name="scales1", align_bytes=64)
        quantize(codes1[:], scales1[:], grouped1[:])
        acc1 = multiply("acc1", C, w_codes1, w_scales1, 0, codes1[:], scales1[:])
        codes3a = keep.tile([P, H], U32, name="codes3a", tag="after_q1", align_bytes=64)
        scales3a = keep.tile([P, H], U8, name="scales3a", align_bytes=64)
        quantize(codes3a[:], scales3a[:], grouped3a[:])

        w_grouped23 = keep.tile([P, 2, N, PACK], BF16, name="w_grouped23", align_bytes=64)
        interleave_weights((nc.vector.tensor_copy, nc.scalar.copy), 1, w_grouped23)
        late = keep.tile([P, (C + H) * PACK], BF16, name="grouped_late", tag="after_w3", align_bytes=64)
        grouped2 = late[:, 0 : C * PACK]
        grouped3b = late[:, C * PACK : (C + H) * PACK]
        sums0 = keep.tile([P, C], F32, name="sums0", tag="after_sc0", align_bytes=64)
        nc.vector.tensor_copy(sums0[:], acc0[:])
        scalar_gather(grouped2, 0, 2 * C, C)
        sums1 = keep.tile([P, C], F32, name="sums1", tag="after_sc1", align_bytes=64)
        nc.scalar.copy(sums1[:], acc1[:])
        for t in range(1, PACK):
            scalar_gather(grouped2, t, 2 * C, C)

        w_codes23 = keep.tile([P, 2 * N], U32, name="w_codes23", align_bytes=64)
        w_scales23 = keep.tile([P, 2 * N], U8, name="w_scales23", align_bytes=64)
        quantize(w_codes23[:], w_scales23[:], w_grouped23[:].rearrange("p e n j -> p (e n j)"))
        acc3a = multiply("acc3a", H, w_codes23, w_scales23, 1, codes3a[:], scales3a[:])
        put_back(sums0[:], 0, C)
        sums3a = keep.tile([P, H], F32, name="sums3a")
        nc.scalar.copy(sums3a[:], acc3a[:])
        for t in range(PACK):
            scalar_gather(grouped3b, t, 3 * C + H, H)
        put_back(sums1[:], C, C)

        codes2 = keep.tile([P, C], U32, name="codes2", tag="after_sc0", align_bytes=64)
        scales2 = keep.tile([P, C], U8, name="scales2", align_bytes=64)
        quantize(codes2[:], scales2[:], grouped2)
        acc2 = multiply("acc2", C, w_codes23, w_scales23, 0, codes2[:], scales2[:])
        put_back(sums3a[:], 3 * C, H)
        codes3b = keep.tile([P, H], U32, name="codes3b", tag="after_sc1", align_bytes=64)
        scales3b = keep.tile([P, H], U8, name="scales3b", align_bytes=64)
        quantize(codes3b[:], scales3b[:], grouped3b)
        acc3b = multiply("acc3b", H, w_codes23, w_scales23, 1, codes3b[:], scales3b[:])
        sums2 = keep.tile([P, C], F32, name="sums2")
        nc.scalar.copy(sums2[:], acc2[:])
        put_back(sums2[:], 2 * C, C)
        sums3b = keep.tile([P, H], F32, name="sums3b")
        nc.scalar.copy(sums3b[:], acc3b[:])
        put_back(sums3b[:], 3 * C + H, H)

        nc.sync.dma_start(out, window[:])
